import numpy as np
import ml_dtypes


def mxq(x, axis, fmt="e4m3"):
    dtype, down = {"e4m3": (ml_dtypes.float8_e4m3fn, 7), "e5m2": (ml_dtypes.float8_e5m2, 14)}[fmt]
    v = np.moveaxis(np.asarray(x, np.float32).astype(ml_dtypes.bfloat16).astype(np.float64), axis, -1)
    blocks = v.reshape(v.shape[:-1] + (-1, 32))
    amax = np.abs(blocks).max(-1, keepdims=True)
    byte = np.maximum(np.where(amax > 0, np.frexp(amax)[1] - 1 + 127, 0) - down, 1)
    scale = np.exp2(byte - 127.0)
    codes = (blocks / scale).astype(np.float32).astype(dtype).astype(np.float64)
    return np.moveaxis((codes * scale).reshape(v.shape), -1, axis)


WIDE = False


def mx_kscale(k):
    if not WIDE:
        return np.ones(k)
    levels = np.array([10, -10, 5, -5, 0])
    if k % 512:
        return np.exp2(np.random.permutation(np.resize(levels, k // 32))).repeat(32)
    a = np.empty((k // 512, 16))
    for p in range(k // 512):
        a[p, :8] = np.random.permutation(np.resize(levels, 8))
        for g in range(8):
            far = levels[np.abs(levels - a[p, g]) >= 10]
            a[p, g + 8] = far[np.random.randint(len(far))]
    return np.exp2(a.ravel()).repeat(32)


def f64(x):
    return np.asarray(x).astype(np.float64)


def striped(idx):
    return np.tile(idx.reshape(-1, 16).T, (8, 1)).astype(np.uint16)


def unstriped(offs):
    return offs[:16].T.reshape(-1).astype(np.int64)


def pack_weight(w):
    k, n = w.shape
    w = f64(np.asarray(w, np.float32).astype(ml_dtypes.bfloat16)).reshape(k // 32, 32, n)
    amax = np.abs(w).max(1)
    byte = np.clip(np.where(amax > 0, np.frexp(amax)[1] - 1 + 127 - 7, 1), 1, 254)
    scaled = (w * np.exp2(127.0 - byte)[:, None, :]).reshape(k, n).astype(np.float32)
    words = np.ascontiguousarray(scaled.reshape(k // 512, 128, 4, n).transpose(0, 1, 3, 2)).astype(ml_dtypes.float8_e4m3fn).view(np.uint8)
    return words, np.ascontiguousarray(byte.astype(np.uint8).reshape(k // 512, 16, n))


def unpack_weight(words, scales):
    g, p, n, _ = words.shape
    vals = np.ascontiguousarray(words).view(ml_dtypes.float8_e4m3fn).astype(np.float64) * np.repeat(np.exp2(scales.astype(np.float64) - 127.0), 8, axis=1)[..., None]
    return vals.transpose(0, 1, 3, 2).reshape(g * 512, n)


def relu(v):
    return np.maximum(v, 0.0)


K, T, D, S, V, N = 1024, 1024, 4, 512, 128, 256


def setup_inputs():
    n = np.random.standard_normal
    s = mx_kscale(K)[:, None]
    words, scales = pack_weight(n((K, N)) / np.sqrt(K) / s)
    return {
        "xT": (n((K, T)) * s).astype(np.float32),
        "w_words": words,
        "w_scales": scales,
        "b": (0.3 * n((N, 1))).astype(np.float32),
        "offs": striped(np.random.permutation(T)[:S]),
    }


def reference(xT, w_words, w_scales, b, offs):
    w = unpack_weight(w_words, w_scales)
    idx = unstriped(offs)
    xq = mxq(f64(xT)[:, idx], 0, "e4m3")
    y = w.T @ xq
    y = relu(y + f64(b))
    return y.reshape(N, V, D).max(axis=2)

@@ -1,0 +1,139 @@
+from contextlib import ExitStack
+
+import concourse.mybir as mybir
+
+K, T, S, V, D, N = 1024, 1024, 512, 128, 4, 256
+P = 128
+PACK = 4
+PASSES = K // (P * PACK)
+PIECES = ((0, 256), (256, 384), (384, 512))
+FLOPS = 2 * K * S * N
+
+F32 = mybir.dt.float32
+BF16 = mybir.dt.bfloat16
+U32 = mybir.dt.uint32
+I32 = mybir.dt.int32
+U16 = mybir.dt.uint16
+U8 = mybir.dt.uint8
+FP8X4 = mybir.dt.float8_e4m3fn_x4
+COPY = mybir.ActivationFunctionType.Copy
+
+
+def tile_picked_pool_lin_relu_sub_e_kernel(tc, xT, w_words, w_scales, b, offs, out):
+    nc = tc.nc
+    with ExitStack() as ctx:
+        keep = ctx.enter_context(tc.tile_pool(name="keep", bufs=1))
+        psum = ctx.enter_context(tc.psum_pool(name="psum", bufs=1))
+
+        lists = keep.tile([P, S // 16], U16, name="lists")
+        nc.sync.dma_start(lists[:], offs)
+
+        planes = xT.rearrange("(a p t) w -> a t p w", a=PASSES, t=PACK)
+        x = {}
+        for a in range(PASSES):
+            for t in range(PACK):
+                x[a, t] = keep.tile([P, T], F32, align_bytes=64, name="x%d%d" % (a, t), tag="x%d%d" % (a, t))
+        wsc = keep.tile([P, N], U8, align_bytes=64, name="wsc")
+        nc.gpsimd.memset(wsc[:].bitcast(I32), 0)
+        words = keep.tile([P, PASSES, N * 4], U8, align_bytes=64, name="words")
+        bias = [keep.tile([P, 1], F32, name="bias%d" % m) for m in range(2)]
+        for t in range(PACK):
+            nc.sync.dma_start(x[0, t][:], planes[0, t])
+            if t == 0:
+                for q in range(4):
+                    nc.sync.dma_start(wsc[32 * q : 32 * q + 8, :].bitcast(I32), w_scales[:, 4 * q : 4 * q + 4, :].bitcast(I32))
+        for t in range(PACK):
+            nc.sync.dma_start(x[1, t][:], planes[1, t])
+        nc.sync.dma_start(words[:, 0, :], w_words[0].rearrange("p n r -> p (n r)"))
+        nc.sync.dma_start(words[:, 1, :], w_words[1].rearrange("p n r -> p (n r)"))
+        for m in range(2):
+            nc.sync.dma_start(bias[m][:], b[m * P : (m + 1) * P, :])
+
+        codes = {1: keep.tile([P, S], U32, align_bytes=64, name="codes1")}
+        scales = [keep.tile([P, S], U8, align_bytes=64, name="scales%d" % a) for a in range(PASSES)]
+        grouped = [keep.tile([P, S, PACK], BF16, align_bytes=64, name="grouped%d" % a) for a in range(PASSES)]
+        paired = [keep.tile([P, 2, S, 2], BF16, align_bytes=64, name="paired%d" % a) for a in range(PASSES)]
+        xb = [keep.tile([P, T], BF16, align_bytes=64, name="xb%d" % t) for t in range(2)]
+        acc = {}
+        for i, (lo, hi) in enumerate(PIECES):
+            for m in range(2):
+                acc[m, i] = psum.tile([P, hi - lo], F32, name="acc%d%d" % (m, i))
+
+        def gather(a, t, lo=0, hi=S):
+            nc.vector.tensor_copy(
+                paired[a][:, t // 2, lo:hi, t % 2],
+                x[a, t][:].indirect(lists[:, lo // 16 : hi // 16]),
+            )
+
+        def merge(copy, a, lo=0, hi=S):
+            dst = grouped[a][:].rearrange("p n t -> p (n t)").bitcast(F32).rearrange("p (n u) -> p n u", u=2)
+            src = paired[a][:].rearrange("p u n e -> p (u n e)").bitcast(F32).rearrange("p (u n) -> p n u", u=2)
+            copy(dst[:, lo:hi, :], src[:, lo:hi, :])
+
+        def quantize(a, lo=0, hi=S):
+            nc.vector.quantize_mx(
+                out=codes[a][:, lo:hi].bitcast(FP8X4),
+                scales=scales[a][:, lo:hi],
+                in_=grouped[a][:, lo:hi, :].rearrange("p n t -> p (n t)"),
+            )
+
+        def product(a, m, i):
+            cols = slice(*PIECES[i])
+            nc.tensor.matmul_mx(
+                out=acc[m, i][:],
+                lhsT=words[:, a, m * P * 4 : (m + 1) * P * 4].bitcast(FP8X4),
+                lhsT_scale=wsc[4 * a :, m * P : (m + 1) * P],
+                rhs=codes[a][:, cols].bitcast(FP8X4),
+                rhs_scale=scales[a][:, cols],
+                start=(a == 0),
+                stop=(a == PASSES - 1),
+            )
+
+        for t in range(PACK):
+            gather(0, t)
+        merge(nc.scalar.copy, 0)
+        for t in range(2):
+            nc.vector.tensor_copy(xb[t][:], x[1, t][:])
+            nc.scalar.activation(paired[1][:, 0, :, t], xb[t][:].indirect(lists[:]), COPY)
+        codes[0] = keep.tile([P, S], U32, align_bytes=64, name="codes0", tag="x11")
+        quantize(0)
+        for i in range(3):
+            for m in range(2):
+                product(0, m, i)
+        gather(1, 2)
+        gather(1, 3, *PIECES[0])
+        gather(1, 3, *PIECES[1])
+        merge(nc.vector.tensor_copy, 1, *PIECES[0])
+        gather(1, 3, *PIECES[2])
+        quantize(1, *PIECES[0])
+        merge(nc.vector.tensor_copy, 1, *PIECES[1])
+        merge(nc.vector.tensor_copy, 1, *PIECES[2])
+        quantize(1, *PIECES[1])
+        quantize(1, *PIECES[2])
+        for i in range(3):
+            for m in range(2):
+                product(1, m, i)
+        best = [keep.tile([P, 2, V // 2], F32, name="best%d" % h) for h in range(2)]
+        result = {(h, m): keep.tile([P, V // 2], F32, name="result%d%d" % (h, m)) for h in range(2) for m in range(2)}
+        for i, (lo, hi) in enumerate(PIECES):
+            h = lo * 2 // S
+            v0 = lo // D - h * V // 2
+            for m in range(2):
+                nc.vector.tensor_reduce(
+                    best[h][:, m, v0 : v0 + (hi - lo) // D],
+                    acc[m, i][:].rearrange("p (v d) -> p v d", d=D),
+                    axis=mybir.AxisListType.X,
+                    op=mybir.AluOpType.max,
+                )
+            if i == 1:
+                continue
+            for m in range(2):
+                nc.vector.tensor_scalar(
+                    result[h, m][:],
+                    best[h][:, m, :],
+                    scalar1=bias[m][:],
+                    scalar2=0.0,
+                    op0=mybir.AluOpType.add,
+                    op1=mybir.AluOpType.max,
+                )
+                nc.sync.dma_start(out[m * P : (m + 1) * P, h * V // 2 : (h + 1) * V // 2], result[h, m][:])

@@ -6,7 +6,8 @@ K, T, S, V, D, N = 1024, 1024, 512, 128, 4, 256
 P = 128
 PACK = 4
 PASSES = K // (P * PACK)
-PIECES = ((0, 256), (256, 384), (384, 512))
+PIECE = 128
+PIECES = tuple((lo, lo + PIECE) for lo in range(0, S, PIECE))
 FLOPS = 2 * K * S * N
 
 F32 = mybir.dt.float32
@@ -17,6 +18,7 @@ U16 = mybir.dt.uint16
 U8 = mybir.dt.uint8
 FP8X4 = mybir.dt.float8_e4m3fn_x4
 COPY = mybir.ActivationFunctionType.Copy
+RELU = mybir.ActivationFunctionType.Relu
 
 
 def tile_picked_pool_lin_relu_sub_e_kernel(tc, xT, w_words, w_scales, b, offs, out):
@@ -49,10 +51,17 @@ def tile_picked_pool_lin_relu_sub_e_kernel(tc, xT, w_words, w_scales, b, offs, o
         for m in range(2):
             nc.sync.dma_start(bias[m][:], b[m * P : (m + 1) * P, :])
 
-        codes = {1: keep.tile([P, S], U32, align_bytes=64, name="codes1")}
-        scales = [keep.tile([P, S], U8, align_bytes=64, name="scales%d" % a) for a in range(PASSES)]
-        grouped = [keep.tile([P, S, PACK], BF16, align_bytes=64, name="grouped%d" % a) for a in range(PASSES)]
+        spans = {0: ((0, S),), 1: PIECES}
+        halves = ((0, S // 2), (S // 2, S))
         paired = [keep.tile([P, 2, S, 2], BF16, align_bytes=64, name="paired%d" % a) for a in range(PASSES)]
+        grouped, codes, scales = {}, {}, {}
+        for a in range(PASSES):
+            for lo, hi in spans[a]:
+                name = "grouped%d_%d" % (a, lo)
+                grouped[a, lo] = keep.tile([P, hi - lo, PACK], BF16, align_bytes=64, name=name, tag=name)
+                scales[a, lo] = keep.tile([P, hi - lo], U8, align_bytes=64, name="scales%d_%d" % (a, lo))
+        for lo, hi in PIECES:
+            codes[1, lo] = keep.tile([P, hi - lo], U32, align_bytes=64, name="codes1_%d" % lo)
         xb = [keep.tile([P, T], BF16, align_bytes=64, name="xb%d" % t) for t in range(2)]
         acc = {}
         for i, (lo, hi) in enumerate(PIECES):
@@ -65,75 +74,78 @@ def tile_picked_pool_lin_relu_sub_e_kernel(tc, xT, w_words, w_scales, b, offs, o
                 x[a, t][:].indirect(lists[:, lo // 16 : hi // 16]),
             )
 
-        def merge(copy, a, lo=0, hi=S):
-            dst = grouped[a][:].rearrange("p n t -> p (n t)").bitcast(F32).rearrange("p (n u) -> p n u", u=2)
+        def merge(a, lo, hi):
+            base = 0 if a == 0 else lo
+            dst = grouped[a, base][:, lo - base : hi - base, :].rearrange("p n t -> p (n t)").bitcast(F32).rearrange("p (n u) -> p n u", u=2)
             src = paired[a][:].rearrange("p u n e -> p (u n e)").bitcast(F32).rearrange("p (u n) -> p n u", u=2)
-            copy(dst[:, lo:hi, :], src[:, lo:hi, :])
+            nc.scalar.copy(dst, src[:, lo:hi, :])
 
-        def quantize(a, lo=0, hi=S):
+        def quantize(a, lo):
             nc.vector.quantize_mx(
-                out=codes[a][:, lo:hi].bitcast(FP8X4),
-                scales=scales[a][:, lo:hi],
-                in_=grouped[a][:, lo:hi, :].rearrange("p n t -> p (n t)"),
+                out=codes[a, lo][:].bitcast(FP8X4),
+                scales=scales[a, lo][:],
+                in_=grouped[a, lo][:].rearrange("p n t -> p (n t)"),
             )
 
         def product(a, m, i):
-            cols = slice(*PIECES[i])
+            lo, hi = PIECES[i]
+            base = 0 if a == 0 else lo
+            cols = slice(lo - base, hi - base)
             nc.tensor.matmul_mx(
                 out=acc[m, i][:],
                 lhsT=words[:, a, m * P * 4 : (m + 1) * P * 4].bitcast(FP8X4),
                 lhsT_scale=wsc[4 * a :, m * P : (m + 1) * P],
-                rhs=codes[a][:, cols].bitcast(FP8X4),
-                rhs_scale=scales[a][:, cols],
+                rhs=codes[a, base][:, cols].bitcast(FP8X4),
+                rhs_scale=scales[a, base][:, cols],
                 start=(a == 0),
                 stop=(a == PASSES - 1),
             )
 
-        for t in range(PACK):
+        for t in range(PACK - 1):
             gather(0, t)
-        merge(nc.scalar.copy, 0)
+        for lo, hi in halves:
+            gather(0, PACK - 1, lo, hi)
+            merge(0, lo, hi)
         for t in range(2):
             nc.vector.tensor_copy(xb[t][:], x[1, t][:])
             nc.scalar.activation(paired[1][:, 0, :, t], xb[t][:].indirect(lists[:]), COPY)
-        codes[0] = keep.tile([P, S], U32, align_bytes=64, name="codes0", tag="x11")
-        quantize(0)
-        for i in range(3):
+        codes[0, 0] = keep.tile([P, S], U32, align_bytes=64, name="codes0", tag="x10")
+        quantize(0, 0)
+        for i in range(len(PIECES)):
             for m in range(2):
                 product(0, m, i)
         gather(1, 2)
-        gather(1, 3, *PIECES[0])
-        gather(1, 3, *PIECES[1])
-        merge(nc.vector.tensor_copy, 1, *PIECES[0])
-        gather(1, 3, *PIECES[2])
-        quantize(1, *PIECES[0])
-        merge(nc.vector.tensor_copy, 1, *PIECES[1])
-        merge(nc.vector.tensor_copy, 1, *PIECES[2])
-        quantize(1, *PIECES[1])
-        quantize(1, *PIECES[2])
-        for i in range(3):
+        for lo, hi in PIECES:
+            gather(1, 3, lo, hi)
+            merge(1, lo, hi)
+        for i, (lo, hi) in enumerate(PIECES):
+            quantize(1, lo)
             for m in range(2):
                 product(1, m, i)
-        best = [keep.tile([P, 2, V // 2], F32, name="best%d" % h) for h in range(2)]
-        result = {(h, m): keep.tile([P, V // 2], F32, name="result%d%d" % (h, m)) for h in range(2) for m in range(2)}
-        for i, (lo, hi) in enumerate(PIECES):
-            h = lo * 2 // S
-            v0 = lo // D - h * V // 2
+        best = keep.tile([P, 2, V], F32, align_bytes=64, name="best", tag="grouped1_%d" % PIECES[-1][0])
+        stores = ((0, 2), (2, 3), (3, 4))
+        for first, last in stores:
+            for i in range(first, last):
+                lo, hi = PIECES[i]
+                for m in range(2):
+                    nc.vector.tensor_reduce(
+                        best[:, m, lo // D : hi // D],
+                        acc[m, i][:].rearrange("p (v d) -> p v d", d=D),
+                        axis=mybir.AxisListType.X,
+                        op=mybir.AluOpType.max,
+                    )
+            centres = slice(first * PIECE // D, last * PIECE // D)
+            result = keep.tile([P, 2, (last - first) * PIECE // D], F32, name="result%d" % first)
             for m in range(2):
-                nc.vector.tensor_reduce(
-                    best[h][:, m, v0 : v0 + (hi - lo) // D],
-                    acc[m, i][:].rearrange("p (v d) -> p v d", d=D),
-                    axis=mybir.AxisListType.X,
-                    op=mybir.AluOpType.max,
-                )
-            if i == 1:
-                continue
-            for m in range(2):
-                nc.vector.tensor_scalar(
-                    result[h, m][:],
-                    best[h][:, m, :],
-                    scalar1=bias[m][:],
-                    scalar2=0.0,
-                    op0=mybir.AluOpType.add,
-                    op1=mybir.AluOpType.max,
-                )
-                nc.sync.dma_start(out[m * P : (m + 1) * P, h * V // 2 : (h + 1) * V // 2], result[h, m][:])
+                if last < len(PIECES):
+                    nc.scalar.activation(result[:, m, :], best[:, m, centres], RELU, bias=bias[m][:])
+                else:
+                    nc.vector.tensor_scalar(
+                        result[:, m, :],
+                        best[:, m, centres],
+                        scalar1=bias[m][:],
+                        scalar2=0.0,
+                        op0=mybir.AluOpType.add,
+                        op1=mybir.AluOpType.max,
+                    )
+            nc.sync.dma_start(out.rearrange("(m p) v -> p m v", m=2)[:, :, centres], result[:])

@@ -39,13 +39,11 @@ def tile_picked_pool_lin_relu_sub_e_kernel(tc, xT, w_words, w_scales, b, offs, o
         nc.gpsimd.memset(wsc[:].bitcast(I32), 0)
         words = keep.tile([P, PASSES, N * 4], U8, align_bytes=64, name="words")
         bias = [keep.tile([P, 1], F32, name="bias%d" % m) for m in range(2)]
-        for t in range(PACK):
-            nc.sync.dma_start(x[0, t][:], planes[0, t])
-            if t == 0:
-                for q in range(4):
-                    nc.sync.dma_start(wsc[32 * q : 32 * q + 8, :].bitcast(I32), w_scales[:, 4 * q : 4 * q + 4, :].bitcast(I32))
-        for t in range(PACK):
-            nc.sync.dma_start(x[1, t][:], planes[1, t])
+        for a in range(PASSES):
+            for t in range(PACK):
+                nc.sync.dma_start(x[a, t][:], planes[a, t])
+        for q in range(4):
+            nc.sync.dma_start(wsc[32 * q : 32 * q + 8, :].bitcast(I32), w_scales[:, 4 * q : 4 * q + 4, :].bitcast(I32))
         nc.sync.dma_start(words[:, 0, :], w_words[0].rearrange("p n r -> p (n r)"))
         nc.sync.dma_start(words[:, 1, :], w_words[1].rearrange("p n r -> p (n r)"))
         for m in range(2):
@@ -122,7 +120,7 @@ def tile_picked_pool_lin_relu_sub_e_kernel(tc, xT, w_words, w_scales, b, offs, o
             quantize(1, lo)
             for m in range(2):
                 product(1, m, i)
-        best = keep.tile([P, 2, V], F32, align_bytes=64, name="best", tag="grouped1_%d" % PIECES[-1][0])
+        best = keep.tile([P, 2, V], F32, align_bytes=64, name="best", tag="grouped1_%d" % PIECES[-2][0])
         stores = ((0, 2), (2, 3), (3, 4))
         for first, last in stores:
             for i in range(first, last):

@@ -8,6 +8,7 @@ PACK = 4
 PASSES = K // (P * PACK)
 PIECE = 128
 PIECES = tuple((lo, lo + PIECE) for lo in range(0, S, PIECE))
+LAST = len(PIECES) - 1
 FLOPS = 2 * K * S * N
 
 F32 = mybir.dt.float32
@@ -63,8 +64,11 @@ def tile_picked_pool_lin_relu_sub_e_kernel(tc, xT, w_words, w_scales, b, offs, o
         xb = [keep.tile([P, T], BF16, align_bytes=64, name="xb%d" % t) for t in range(2)]
         acc = {}
         for i, (lo, hi) in enumerate(PIECES):
-            for m in range(2):
-                acc[m, i] = psum.tile([P, hi - lo], F32, name="acc%d%d" % (m, i))
+            if i < LAST:
+                shared = psum.tile([P, 2, hi - lo], F32, name="acc%d" % i)
+                acc[i] = [shared[:, 0, :], shared[:, 1, :], shared[:]]
+            else:
+                acc[i] = [psum.tile([P, hi - lo], F32, name="acc%d%d" % (i, m))[:] for m in range(2)]
 
         def gather(a, t, lo=0, hi=S):
             nc.vector.tensor_copy(
@@ -72,11 +76,11 @@ def tile_picked_pool_lin_relu_sub_e_kernel(tc, xT, w_words, w_scales, b, offs, o
                 x[a, t][:].indirect(lists[:, lo // 16 : hi // 16]),
             )
 
-        def merge(a, lo, hi):
+        def merge(a, lo, hi, copy=nc.scalar.copy):
             base = 0 if a == 0 else lo
-            dst = grouped[a, base][:, lo - base : hi - base, :].rearrange("p n t -> p (n t)").bitcast(F32).rearrange("p (n u) -> p n u", u=2)
-            src = paired[a][:].rearrange("p u n e -> p (u n e)").bitcast(F32).rearrange("p (u n) -> p n u", u=2)
-            nc.scalar.copy(dst, src[:, lo:hi, :])
+            dst = grouped[a, base][:, lo - base : hi - base, :].rearrange("p n t -> p (n t)").bitcast(U32).rearrange("p (n u) -> p n u", u=2)
+            src = paired[a][:].rearrange("p u n e -> p (u n e)").bitcast(U32).rearrange("p (u n) -> p n u", u=2)
+            copy(dst, src[:, lo:hi, :])
 
         def quantize(a, lo):
             nc.vector.quantize_mx(
@@ -90,13 +94,13 @@ def tile_picked_pool_lin_relu_sub_e_kernel(tc, xT, w_words, w_scales, b, offs, o
             base = 0 if a == 0 else lo
             cols = slice(lo - base, hi - base)
             nc.tensor.matmul_mx(
-                out=acc[m, i][:],
+                out=acc[i][m],
                 lhsT=words[:, a, m * P * 4 : (m + 1) * P * 4].bitcast(FP8X4),
                 lhsT_scale=wsc[4 * a :, m * P : (m + 1) * P],
                 rhs=codes[a, base][:, cols].bitcast(FP8X4),
                 rhs_scale=scales[a, base][:, cols],
-                start=(a == 0),
-                stop=(a == PASSES - 1),
+                start=(a == 0 and (m == 0 or i == LAST)),
+                stop=(a == PASSES - 1 and (m == 1 or i == LAST)),
             )
 
         for t in range(PACK - 1):
@@ -113,9 +117,9 @@ def tile_picked_pool_lin_relu_sub_e_kernel(tc, xT, w_words, w_scales, b, offs, o
             for m in range(2):
                 product(0, m, i)
         gather(1, 2)
-        for lo, hi in PIECES:
+        for i, (lo, hi) in enumerate(PIECES):
             gather(1, 3, lo, hi)
-            merge(1, lo, hi)
+            merge(1, lo, hi, nc.gpsimd.tensor_copy if i == 0 else nc.scalar.copy)
         for i, (lo, hi) in enumerate(PIECES):
             quantize(1, lo)
             for m in range(2):
@@ -125,13 +129,21 @@ def tile_picked_pool_lin_relu_sub_e_kernel(tc, xT, w_words, w_scales, b, offs, o
         for first, last in stores:
             for i in range(first, last):
                 lo, hi = PIECES[i]
-                for m in range(2):
+                if i < LAST:
                     nc.vector.tensor_reduce(
-                        best[:, m, lo // D : hi // D],
-                        acc[m, i][:].rearrange("p (v d) -> p v d", d=D),
+                        best[:, :, lo // D : hi // D],
+                        acc[i][2].rearrange("p m (v d) -> p m v d", d=D),
                         axis=mybir.AxisListType.X,
                         op=mybir.AluOpType.max,
                     )
+                else:
+                    for m in range(2):
+                        nc.vector.tensor_reduce(
+                            best[:, m, lo // D : hi // D],
+                            acc[i][m].rearrange("p (v d) -> p v d", d=D),
+                            axis=mybir.AxisListType.X,
+                            op=mybir.AluOpType.max,
+                        )
             centres = slice(first * PIECE // D, last * PIECE // D)
             result = keep.tile([P, 2, (last - first) * PIECE // D], F32, name="result%d" % first)
             for m in range(2):

@@ -7,8 +7,9 @@ P = 128
 PACK = 4
 PASSES = K // (P * PACK)
 PIECE = 128
-PIECES = tuple((lo, lo + PIECE) for lo in range(0, S, PIECE))
-LAST = len(PIECES) - 1
+HALF = S // 2
+PIECES = S // PIECE
+LAST = PIECES - 1
 FLOPS = 2 * K * S * N
 
 F32 = mybir.dt.float32
@@ -32,55 +33,74 @@ def tile_picked_pool_lin_relu_sub_e_kernel(tc, xT, w_words, w_scales, b, offs, o
         nc.sync.dma_start(lists[:], offs)
 
         planes = xT.rearrange("(a p t) w -> a t p w", a=PASSES, t=PACK)
-        x = {}
+        plane = {}
         for a in range(PASSES):
             for t in range(PACK):
-                x[a, t] = keep.tile([P, T], F32, align_bytes=64, name="x%d%d" % (a, t), tag="x%d%d" % (a, t))
+                x = keep.tile([P, T], F32, align_bytes=64, name="x%d%d" % (a, t))
+                nc.sync.dma_start(x[:], planes[a, t])
+                plane[a, t] = x[:]
         wsc = keep.tile([P, N], U8, align_bytes=64, name="wsc")
         nc.gpsimd.memset(wsc[:].bitcast(I32), 0)
+        early = keep.tile([P, 2], F32, name="early")
+        nc.gpsimd.memset(early[:, 0:1], 0.0)
+        nc.scalar.activation(early[:, 1:2], early[:, 0:1], COPY)
         words = keep.tile([P, PASSES, N * 4], U8, align_bytes=64, name="words")
         bias = [keep.tile([P, 1], F32, name="bias%d" % m) for m in range(2)]
-        for a in range(PASSES):
-            for t in range(PACK):
-                nc.sync.dma_start(x[a, t][:], planes[a, t])
         for q in range(4):
             nc.sync.dma_start(wsc[32 * q : 32 * q + 8, :].bitcast(I32), w_scales[:, 4 * q : 4 * q + 4, :].bitcast(I32))
-        nc.sync.dma_start(words[:, 0, :], w_words[0].rearrange("p n r -> p (n r)"))
-        nc.sync.dma_start(words[:, 1, :], w_words[1].rearrange("p n r -> p (n r)"))
+        for a in range(PASSES):
+            nc.sync.dma_start(words[:, a, :], w_words[a].rearrange("p n r -> p (n r)"))
         for m in range(2):
             nc.sync.dma_start(bias[m][:], b[m * P : (m + 1) * P, :])
 
-        spans = {0: ((0, S),), 1: PIECES}
-        halves = ((0, S // 2), (S // 2, S))
-        paired = [keep.tile([P, 2, S, 2], BF16, align_bytes=64, name="paired%d" % a) for a in range(PASSES)]
+        width = {0: HALF, 1: PIECE}
         grouped, codes, scales = {}, {}, {}
         for a in range(PASSES):
-            for lo, hi in spans[a]:
+            for lo in range(0, S, width[a]):
                 name = "grouped%d_%d" % (a, lo)
-                grouped[a, lo] = keep.tile([P, hi - lo, PACK], BF16, align_bytes=64, name=name, tag=name)
-                scales[a, lo] = keep.tile([P, hi - lo], U8, align_bytes=64, name="scales%d_%d" % (a, lo))
-        for lo, hi in PIECES:
-            codes[1, lo] = keep.tile([P, hi - lo], U32, align_bytes=64, name="codes1_%d" % lo)
-        xb = [keep.tile([P, T], BF16, align_bytes=64, name="xb%d" % t) for t in range(2)]
+                grouped[a, lo] = keep.tile([P, width[a], PACK], BF16, align_bytes=64, name=name, tag=name)
+                codes[a, lo] = keep.tile([P, width[a]], U32, align_bytes=64, name="codes%d_%d" % (a, lo))
+                scales[a, lo] = keep.tile([P, width[a]], U8, align_bytes=64, name="scales%d_%d" % (a, lo))
+        paired = [keep.tile([P, HALF // width[a], 2, width[a], 2], BF16, align_bytes=64, name="paired%d" % a) for a in range(PASSES)]
+        rows0 = keep.tile([P, PACK, HALF], BF16, align_bytes=64, name="rows0")
+        rows = [
+            keep.tile([P, 1, 2, HALF], BF16, align_bytes=64, name="rows10"),
+            keep.tile([P, HALF // PIECE, 2, PIECE], BF16, align_bytes=64, name="rows11"),
+        ]
         acc = {}
-        for i, (lo, hi) in enumerate(PIECES):
+        for i in range(PIECES):
             if i < LAST:
-                shared = psum.tile([P, 2, hi - lo], F32, name="acc%d" % i)
+                shared = psum.tile([P, 2, PIECE], F32, name="acc%d" % i)
                 acc[i] = [shared[:, 0, :], shared[:, 1, :], shared[:]]
             else:
-                acc[i] = [psum.tile([P, hi - lo], F32, name="acc%d%d" % (i, m))[:] for m in range(2)]
+                acc[i] = [psum.tile([P, PIECE], F32, name="acc%d%d" % (i, m))[:] for m in range(2)]
 
-        def gather(a, t, lo=0, hi=S):
-            nc.vector.tensor_copy(
-                paired[a][:, t // 2, lo:hi, t % 2],
-                x[a, t][:].indirect(lists[:, lo // 16 : hi // 16]),
-            )
+        def offsets(lo, hi):
+            return lists[:, lo // 16 : hi // 16]
 
-        def merge(a, lo, hi, copy=nc.scalar.copy):
-            base = 0 if a == 0 else lo
-            dst = grouped[a, base][:, lo - base : hi - base, :].rearrange("p n t -> p (n t)").bitcast(U32).rearrange("p (n u) -> p n u", u=2)
-            src = paired[a][:].rearrange("p u n e -> p (u n e)").bitcast(U32).rearrange("p (u n) -> p n u", u=2)
-            copy(dst, src[:, lo:hi, :])
+        def gather_pairs(a, t, lo=0, hi=HALF):
+            w = width[a]
+            nc.vector.tensor_copy(paired[a][:, lo // w : hi // w, t // 2, :, t % 2], plane[a, t].indirect(offsets(lo, hi)))
+
+        def gather_rows(a, t):
+            if a == 0:
+                nc.scalar.activation(rows0[:, t, :], plane[a, t].indirect(offsets(HALF, S)), COPY)
+                return
+            tile = rows[t // 2]
+            w = tile.shape[3]
+            for j in range(HALF // w):
+                lo = HALF + j * w
+                nc.scalar.activation(tile[:, j, t % 2, :], plane[a, t].indirect(offsets(lo, lo + w)), COPY)
+
+        def merge(a, lo):
+            dst = grouped[a, lo][:].rearrange("p n t -> p (n t)").bitcast(U32).rearrange("p (n u) -> p n u", u=2)
+            src = paired[a][:, lo // width[a]].rearrange("p u n e -> p (u n e)").bitcast(U32).rearrange("p (u n) -> p n u", u=2)
+            nc.vector.tensor_copy(dst, src)
+
+        def weave(u, lo, copy):
+            tile = rows[u]
+            j, c = divmod(lo - HALF, tile.shape[3])
+            copy(grouped[1, lo][:, :, 2 * u : 2 * u + 2], tile[:, j, :, c : c + PIECE].rearrange("p e n -> p n e"))
 
         def quantize(a, lo):
             nc.vector.quantize_mx(
@@ -90,9 +110,8 @@ def tile_picked_pool_lin_relu_sub_e_kernel(tc, xT, w_words, w_scales, b, offs, o
             )
 
         def product(a, m, i):
-            lo, hi = PIECES[i]
-            base = 0 if a == 0 else lo
-            cols = slice(lo - base, hi - base)
+            base = i * PIECE // width[a] * width[a]
+            cols = slice(i * PIECE - base, (i + 1) * PIECE - base)
             nc.tensor.matmul_mx(
                 out=acc[i][m],
                 lhsT=words[:, a, m * P * 4 : (m + 1) * P * 4].bitcast(FP8X4),
@@ -103,35 +122,39 @@ def tile_picked_pool_lin_relu_sub_e_kernel(tc, xT, w_words, w_scales, b, offs, o
                 stop=(a == PASSES - 1 and (m == 1 or i == LAST)),
             )
 
-        for t in range(PACK - 1):
-            gather(0, t)
-        for lo, hi in halves:
-            gather(0, PACK - 1, lo, hi)
-            merge(0, lo, hi)
-        for t in range(2):
-            nc.vector.tensor_copy(xb[t][:], x[1, t][:])
-            nc.scalar.activation(paired[1][:, 0, :, t], xb[t][:].indirect(lists[:]), COPY)
-        codes[0, 0] = keep.tile([P, S], U32, align_bytes=64, name="codes0", tag="x10")
-        quantize(0, 0)
-        for i in range(len(PIECES)):
-            for m in range(2):
-                product(0, m, i)
-        gather(1, 2)
-        for i, (lo, hi) in enumerate(PIECES):
-            gather(1, 3, lo, hi)
-            merge(1, lo, hi, nc.gpsimd.tensor_copy if i == 0 else nc.scalar.copy)
-        for i, (lo, hi) in enumerate(PIECES):
-            quantize(1, lo)
-            for m in range(2):
-                product(1, m, i)
-        best = keep.tile([P, 2, V], F32, align_bytes=64, name="best", tag="grouped1_%d" % PIECES[-2][0])
+        for a in range(PASSES):
+            for t in range(PACK):
+                if a == 1 and t == PACK - 1:
+                    for lo in range(0, HALF, PIECE):
+                        gather_pairs(a, t, lo, lo + PIECE)
+                else:
+                    gather_pairs(a, t)
+                gather_rows(a, t)
+                if a == 1 and t % 2 == 1:
+                    for lo in range(HALF, S, PIECE):
+                        weave(t // 2, lo, nc.vector.tensor_copy if (t, lo) == (1, S - PIECE) else nc.scalar.copy)
+            for lo in range(0, HALF, width[a]):
+                merge(a, lo)
+            if a == 0:
+                for lo, copy in ((0, nc.scalar.copy), (PIECE, nc.vector.tensor_copy)):
+                    copy(
+                        grouped[0, HALF][:, lo : lo + PIECE, :].rearrange("p (c i) t -> p c t i", i=4),
+                        rows0[:, :, lo : lo + PIECE].rearrange("p t (c i) -> p c t i", i=4),
+                    )
+            for lo in range(0, S, width[a]):
+                quantize(a, lo)
+            for i in range(PIECES):
+                for m in range(2):
+                    product(a, m, i)
+
+        best = keep.tile([P, 2, V], F32, align_bytes=64, name="best", tag="grouped1_%d" % ((LAST - 1) * PIECE))
         stores = ((0, 2), (2, 3), (3, 4))
         for first, last in stores:
             for i in range(first, last):
-                lo, hi = PIECES[i]
+                centres = slice(i * PIECE // D, (i + 1) * PIECE // D)
                 if i < LAST:
                     nc.vector.tensor_reduce(
-                        best[:, :, lo // D : hi // D],
+                        best[:, :, centres],
                         acc[i][2].rearrange("p m (v d) -> p m v d", d=D),
                         axis=mybir.AxisListType.X,
                         op=mybir.AluOpType.max,
@@ -139,7 +162,7 @@ def tile_picked_pool_lin_relu_sub_e_kernel(tc, xT, w_words, w_scales, b, offs, o
                 else:
                     for m in range(2):
                         nc.vector.tensor_reduce(
-                            best[:, m, lo // D : hi // D],
+                            best[:, m, centres],
                             acc[i][m].rearrange("p (v d) -> p v d", d=D),
                             axis=mybir.AxisListType.X,
                             op=mybir.AluOpType.max,
@@ -147,7 +170,7 @@ def tile_picked_pool_lin_relu_sub_e_kernel(tc, xT, w_words, w_scales, b, offs, o
             centres = slice(first * PIECE // D, last * PIECE // D)
             result = keep.tile([P, 2, (last - first) * PIECE // D], F32, name="result%d" % first)
             for m in range(2):
-                if last < len(PIECES):
+                if last < PIECES:
                     nc.scalar.activation(result[:, m, :], best[:, m, centres], RELU, bias=bias[m][:])
                 else:
                     nc.vector.tensor_scalar(

@@ -39,15 +39,17 @@ def tile_picked_pool_lin_relu_sub_e_kernel(tc, xT, w_words, w_scales, b, offs, o
                 x = keep.tile([P, T], F32, align_bytes=64, name="x%d%d" % (a, t))
                 nc.sync.dma_start(x[:], planes[a, t])
                 plane[a, t] = x[:]
-        wsc = keep.tile([P, N], U8, align_bytes=64, name="wsc")
-        nc.gpsimd.memset(wsc[:].bitcast(I32), 0)
+        packed = keep.tile([P, S], U8, align_bytes=64, name="packed")
+        for q in range(4):
+            nc.scalar.dma_start(
+                packed[32 * q + 4 : 32 * q + 8, :].bitcast(I32).rearrange("r (a n) -> r a n", a=PASSES),
+                w_scales[:, 4 * q : 4 * q + 4, :].bitcast(I32).rearrange("a r n -> r a n"),
+            )
         early = keep.tile([P, 2], F32, name="early")
         nc.gpsimd.memset(early[:, 0:1], 0.0)
         nc.scalar.activation(early[:, 1:2], early[:, 0:1], COPY)
         words = keep.tile([P, PASSES, N * 4], U8, align_bytes=64, name="words")
         bias = [keep.tile([P, 1], F32, name="bias%d" % m) for m in range(2)]
-        for q in range(4):
-            nc.sync.dma_start(wsc[32 * q : 32 * q + 8, :].bitcast(I32), w_scales[:, 4 * q : 4 * q + 4, :].bitcast(I32))
         for a in range(PASSES):
             nc.sync.dma_start(words[:, a, :], w_words[a].rearrange("p n r -> p (n r)"))
         for m in range(2):
@@ -60,7 +62,10 @@ def tile_picked_pool_lin_relu_sub_e_kernel(tc, xT, w_words, w_scales, b, offs, o
                 name = "grouped%d_%d" % (a, lo)
                 grouped[a, lo] = keep.tile([P, width[a], PACK], BF16, align_bytes=64, name=name, tag=name)
                 codes[a, lo] = keep.tile([P, width[a]], U32, align_bytes=64, name="codes%d_%d" % (a, lo))
-                scales[a, lo] = keep.tile([P, width[a]], U8, align_bytes=64, name="scales%d_%d" % (a, lo))
+                if a == 0:
+                    scales[a, lo] = packed[:, lo : lo + HALF]
+                else:
+                    scales[a, lo] = keep.tile([P, width[a]], U8, align_bytes=64, name="scales%d_%d" % (a, lo))[:]
         paired = [keep.tile([P, HALF // width[a], 2, width[a], 2], BF16, align_bytes=64, name="paired%d" % a) for a in range(PASSES)]
         rows0 = keep.tile([P, PACK, HALF], BF16, align_bytes=64, name="rows0")
         rows = [
@@ -105,7 +110,7 @@ def tile_picked_pool_lin_relu_sub_e_kernel(tc, xT, w_words, w_scales, b, offs, o
         def quantize(a, lo):
             nc.vector.quantize_mx(
                 out=codes[a, lo][:].bitcast(FP8X4),
-                scales=scales[a, lo][:],
+                scales=scales[a, lo],
                 in_=grouped[a, lo][:].rearrange("p n t -> p (n t)"),
             )
 
@@ -115,7 +120,7 @@ def tile_picked_pool_lin_relu_sub_e_kernel(tc, xT, w_words, w_scales, b, offs, o
             nc.tensor.matmul_mx(
                 out=acc[i][m],
                 lhsT=words[:, a, m * P * 4 : (m + 1) * P * 4].bitcast(FP8X4),
-                lhsT_scale=wsc[4 * a :, m * P : (m + 1) * P],
+                lhsT_scale=packed[4:, a * N + m * P : a * N + (m + 1) * P],
                 rhs=codes[a, base][:, cols].bitcast(FP8X4),
                 rhs_scale=scales[a, base][:, cols],
                 start=(a == 0 and (m == 0 or i == LAST)),

@@ -30,7 +30,6 @@ def tile_picked_pool_lin_relu_sub_e_kernel(tc, xT, w_words, w_scales, b, offs, o
         psum = ctx.enter_context(tc.psum_pool(name="psum", bufs=1))
 
         lists = keep.tile([P, S // 16], U16, name="lists")
-        nc.sync.dma_start(lists[:], offs)
 
         planes = xT.rearrange("(a p t) w -> a t p w", a=PASSES, t=PACK)
         plane = {}
@@ -39,6 +38,8 @@ def tile_picked_pool_lin_relu_sub_e_kernel(tc, xT, w_words, w_scales, b, offs, o
                 x = keep.tile([P, T], F32, align_bytes=64, name="x%d%d" % (a, t))
                 nc.sync.dma_start(x[:], planes[a, t])
                 plane[a, t] = x[:]
+                if (a, t) == (0, 0):
+                    nc.sync.dma_start(lists[:], offs)
         packed = keep.tile([P, S], U8, align_bytes=64, name="packed")
         for q in range(4):
             nc.scalar.dma_start(

@@ -46,9 +46,6 @@ def tile_picked_pool_lin_relu_sub_e_kernel(tc, xT, w_words, w_scales, b, offs, o
                 packed[32 * q + 4 : 32 * q + 8, :].bitcast(I32).rearrange("r (a n) -> r a n", a=PASSES),
                 w_scales[:, 4 * q : 4 * q + 4, :].bitcast(I32).rearrange("a r n -> r a n"),
             )
-        early = keep.tile([P, 2], F32, name="early")
-        nc.gpsimd.memset(early[:, 0:1], 0.0)
-        nc.scalar.activation(early[:, 1:2], early[:, 0:1], COPY)
         words = keep.tile([P, PASSES, N * 4], U8, align_bytes=64, name="words")
         bias = [keep.tile([P, 1], F32, name="bias%d" % m) for m in range(2)]
         for a in range(PASSES):

@@ -40,11 +40,17 @@ def tile_picked_pool_lin_relu_sub_e_kernel(tc, xT, w_words, w_scales, b, offs, o
                 plane[a, t] = x[:]
                 if (a, t) == (0, 0):
                     nc.sync.dma_start(lists[:], offs)
+        staged = keep.tile([4, PASSES, 4, N // 4], I32, align_bytes=64, name="staged")
+        nc.scalar.dma_start(
+            staged[:].rearrange("r a q n -> r (a q) n"),
+            w_scales.bitcast(I32).rearrange("a (q r) n -> r (a q) n", r=4),
+        )
         packed = keep.tile([P, S], U8, align_bytes=64, name="packed")
         for q in range(4):
-            nc.scalar.dma_start(
-                packed[32 * q + 4 : 32 * q + 8, :].bitcast(I32).rearrange("r (a n) -> r a n", a=PASSES),
-                w_scales[:, 4 * q : 4 * q + 4, :].bitcast(I32).rearrange("a r n -> r a n"),
+            copy, word = (nc.scalar.copy, U32) if q == 0 else (nc.vector.tensor_copy, I32)
+            copy(
+                packed[32 * q : 32 * q + 4, :].bitcast(word).rearrange("r (a n) -> r a n", a=PASSES),
+                staged[:].bitcast(word)[:, :, q, :],
             )
         words = keep.tile([P, PASSES, N * 4], U8, align_bytes=64, name="words")
         bias = [keep.tile([P, 1], F32, name="bias%d" % m) for m in range(2)]
@@ -61,7 +67,7 @@ def tile_picked_pool_lin_relu_sub_e_kernel(tc, xT, w_words, w_scales, b, offs, o
                 grouped[a, lo] = keep.tile([P, width[a], PACK], BF16, align_bytes=64, name=name, tag=name)
                 codes[a, lo] = keep.tile([P, width[a]], U32, align_bytes=64, name="codes%d_%d" % (a, lo))
                 if a == 0:
-                    scales[a, lo] = packed[:, lo : lo + HALF]
+                    scales[a, lo] = packed[4:, lo : lo + HALF]
                 else:
                     scales[a, lo] = keep.tile([P, width[a]], U8, align_bytes=64, name="scales%d_%d" % (a, lo))[:]
         paired = [keep.tile([P, HALF // width[a], 2, width[a], 2], BF16, align_bytes=64, name="paired%d" % a) for a in range(PASSES)]
@@ -118,7 +124,7 @@ def tile_picked_pool_lin_relu_sub_e_kernel(tc, xT, w_words, w_scales, b, offs, o
             nc.tensor.matmul_mx(
                 out=acc[i][m],
                 lhsT=words[:, a, m * P * 4 : (m + 1) * P * 4].bitcast(FP8X4),
-                lhsT_scale=packed[4:, a * N + m * P : a * N + (m + 1) * P],
+                lhsT_scale=packed[:, a * N + m * P : a * N + (m + 1) * P],
                 rhs=codes[a, base][:, cols].bitcast(FP8X4),
                 rhs_scale=scales[a, base][:, cols],
                 start=(a == 0 and (m == 0 or i == LAST)),

@@ -53,11 +53,18 @@ def tile_picked_pool_lin_relu_sub_e_kernel(tc, xT, w_words, w_scales, b, offs, o
                 staged[:].bitcast(word)[:, :, q, :],
             )
         words = keep.tile([P, PASSES, N * 4], U8, align_bytes=64, name="words")
-        bias = [keep.tile([P, 1], F32, name="bias%d" % m) for m in range(2)]
+        lying = keep.tile([P, 64], F32, align_bytes=64, name="lying")
+        standing = keep.tile([P, 64], F32, align_bytes=64, name="standing")
+        nc.gpsimd.memset(lying[:], 0.0)
+        nc.scalar.dma_start(
+            lying[0:P:32, :].rearrange("q (m i) -> q m i", m=2),
+            b.rearrange("(m q i) o -> q m (i o)", m=2, q=4),
+        )
+        for m in range(2):
+            nc.vector.transpose(standing[:, 32 * m : 32 * m + 32], lying[:, 32 * m : 32 * m + 32])
+        bias = [standing[:, 32 * m : 32 * m + 1] for m in range(2)]
         for a in range(PASSES):
             nc.sync.dma_start(words[:, a, :], w_words[a].rearrange("p n r -> p (n r)"))
-        for m in range(2):
-            nc.sync.dma_start(bias[m][:], b[m * P : (m + 1) * P, :])
 
         width = {0: HALF, 1: PIECE}
         grouped, codes, scales = {}, {}, {}
@@ -180,12 +187,12 @@ def tile_picked_pool_lin_relu_sub_e_kernel(tc, xT, w_words, w_scales, b, offs, o
             result = keep.tile([P, 2, (last - first) * PIECE // D], F32, name="result%d" % first)
             for m in range(2):
                 if last < PIECES:
-                    nc.scalar.activation(result[:, m, :], best[:, m, centres], RELU, bias=bias[m][:])
+                    nc.scalar.activation(result[:, m, :], best[:, m, centres], RELU, bias=bias[m])
                 else:
                     nc.vector.tensor_scalar(
                         result[:, m, :],
                         best[:, m, centres],
-                        scalar1=bias[m][:],
+                        scalar1=bias[m],
                         scalar2=0.0,
                         op0=mybir.AluOpType.add,
                         op1=mybir.AluOpType.max,

@@ -83,13 +83,10 @@ def tile_picked_pool_lin_relu_sub_e_kernel(tc, xT, w_words, w_scales, b, offs, o
             keep.tile([P, 1, 2, HALF], BF16, align_bytes=64, name="rows10"),
             keep.tile([P, HALF // PIECE, 2, PIECE], BF16, align_bytes=64, name="rows11"),
         ]
-        acc = {}
-        for i in range(PIECES):
-            if i < LAST:
-                shared = psum.tile([P, 2, PIECE], F32, name="acc%d" % i)
-                acc[i] = [shared[:, 0, :], shared[:, 1, :], shared[:]]
-            else:
-                acc[i] = [psum.tile([P, PIECE], F32, name="acc%d%d" % (i, m))[:] for m in range(2)]
+        banks = [((0, 0),), ((0, 1),), ((1, 0),), ((1, 1),), ((2, 0), (3, 0)), ((2, 1),), ((3, 1),)]
+        bank = []
+        for j, sums in enumerate(banks):
+            bank.append(psum.tile([P, len(sums), PIECE], F32, name="bank%d" % j))
 
         def offsets(lo, hi):
             return lists[:, lo // 16 : hi // 16]
@@ -125,17 +122,17 @@ def tile_picked_pool_lin_relu_sub_e_kernel(tc, xT, w_words, w_scales, b, offs, o
                 in_=grouped[a, lo][:].rearrange("p n t -> p (n t)"),
             )
 
-        def product(a, m, i):
+        def product(a, m, i, target, count, start, stop):
             base = i * PIECE // width[a] * width[a]
-            cols = slice(i * PIECE - base, (i + 1) * PIECE - base)
+            cols = slice(i * PIECE - base, (i + count) * PIECE - base)
             nc.tensor.matmul_mx(
-                out=acc[i][m],
+                out=target,
                 lhsT=words[:, a, m * P * 4 : (m + 1) * P * 4].bitcast(FP8X4),
                 lhsT_scale=packed[:, a * N + m * P : a * N + (m + 1) * P],
                 rhs=codes[a, base][:, cols].bitcast(FP8X4),
                 rhs_scale=scales[a, base][:, cols],
-                start=(a == 0 and (m == 0 or i == LAST)),
-                stop=(a == PASSES - 1 and (m == 1 or i == LAST)),
+                start=start,
+                stop=stop,
             )
 
         for a in range(PASSES):
@@ -159,42 +156,38 @@ def tile_picked_pool_lin_relu_sub_e_kernel(tc, xT, w_words, w_scales, b, offs, o
                     )
             for lo in range(0, S, width[a]):
                 quantize(a, lo)
-            for i in range(PIECES):
-                for m in range(2):
-                    product(a, m, i)
+            for j, sums in enumerate(banks):
+                if a == 0:
+                    i, m = sums[0]
+                    product(a, m, i, bank[j][:].rearrange("p c n -> p (c n)"), len(sums), True, False)
+                else:
+                    for c, (i, m) in enumerate(sums):
+                        product(a, m, i, bank[j][:, c, :], 1, False, c == len(sums) - 1)
 
         best = keep.tile([P, 2, V], F32, align_bytes=64, name="best", tag="grouped1_%d" % ((LAST - 1) * PIECE))
-        stores = ((0, 2), (2, 3), (3, 4))
-        for first, last in stores:
-            for i in range(first, last):
-                centres = slice(i * PIECE // D, (i + 1) * PIECE // D)
-                if i < LAST:
-                    nc.vector.tensor_reduce(
-                        best[:, :, centres],
-                        acc[i][2].rearrange("p m (v d) -> p m v d", d=D),
-                        axis=mybir.AxisListType.X,
-                        op=mybir.AluOpType.max,
-                    )
-                else:
-                    for m in range(2):
-                        nc.vector.tensor_reduce(
-                            best[:, m, centres],
-                            acc[i][m].rearrange("p (v d) -> p v d", d=D),
-                            axis=mybir.AxisListType.X,
-                            op=mybir.AluOpType.max,
-                        )
-            centres = slice(first * PIECE // D, last * PIECE // D)
-            result = keep.tile([P, 2, (last - first) * PIECE // D], F32, name="result%d" % first)
-            for m in range(2):
-                if last < PIECES:
-                    nc.scalar.activation(result[:, m, :], best[:, m, centres], RELU, bias=bias[m])
-                else:
-                    nc.vector.tensor_scalar(
-                        result[:, m, :],
-                        best[:, m, centres],
-                        scalar1=bias[m],
-                        scalar2=0.0,
-                        op0=mybir.AluOpType.add,
-                        op1=mybir.AluOpType.max,
-                    )
-            nc.sync.dma_start(out.rearrange("(m p) v -> p m v", m=2)[:, :, centres], result[:])
+        w = PIECE // D
+        for i, sums in enumerate(banks):
+            first, m = sums[0]
+            nc.vector.tensor_reduce(
+                best[:, m, first * w : (first + len(sums)) * w].rearrange("p (c v) -> p c v", c=len(sums)),
+                bank[i][:].rearrange("p c (v d) -> p c v d", d=D),
+                axis=mybir.AxisListType.X,
+                op=mybir.AluOpType.max,
+            )
+            if i == 3:
+                early = keep.tile([P, 2, V // 2], F32, name="early")
+                for m in range(2):
+                    nc.scalar.activation(early[:, m, :], best[:, m, 0 : V // 2], RELU, bias=bias[m])
+                nc.sync.dma_start(out.rearrange("(m p) v -> p m v", m=2)[:, :, 0 : V // 2], early[:])
+        late = [keep.tile([P, V // 2], F32, name="late%d" % m) for m in range(2)]
+        nc.scalar.activation(late[0][:], best[:, 0, V // 2 : V], RELU, bias=bias[0])
+        nc.vector.tensor_scalar(
+            late[1][:],
+            best[:, 1, V // 2 : V],
+            scalar1=bias[1],
+            scalar2=0.0,
+            op0=mybir.AluOpType.add,
+            op1=mybir.AluOpType.max,
+        )
+        for m in range(2):
+            nc.sync.dma_start(out[m * P : (m + 1) * P, V // 2 : V], late[m][:])

@@ -83,7 +83,7 @@ def tile_picked_pool_lin_relu_sub_e_kernel(tc, xT, w_words, w_scales, b, offs, o
             keep.tile([P, 1, 2, HALF], BF16, align_bytes=64, name="rows10"),
             keep.tile([P, HALF // PIECE, 2, PIECE], BF16, align_bytes=64, name="rows11"),
         ]
-        banks = [((0, 0),), ((0, 1),), ((1, 0),), ((1, 1),), ((2, 0), (3, 0)), ((2, 1),), ((3, 1),)]
+        banks = [((0, 0),), ((0, 1),), ((1, 0),), ((1, 1),), ((2, 0),), ((3, 0),), ((2, 1),), ((3, 1),)]
         bank = []
         for j, sums in enumerate(banks):
             bank.append(psum.tile([P, len(sums), PIECE], F32, name="bank%d" % j))

@@ -35,12 +35,12 @@ def tile_picked_pool_lin_relu_sub_e_kernel(tc, xT, w_words, w_scales, b, offs, o
         plane = {}
         for a in range(PASSES):
             for t in range(PACK):
-                x = keep.tile([P, T], F32, align_bytes=64, name="x%d%d" % (a, t))
+                x = keep.tile([P, T], F32, align_bytes=256, name="x%d%d" % (a, t))
                 nc.sync.dma_start(x[:], planes[a, t])
                 plane[a, t] = x[:]
                 if (a, t) == (0, 0):
                     nc.sync.dma_start(lists[:], offs)
-        staged = keep.tile([4, PASSES, 4, N // 4], I32, align_bytes=64, name="staged")
+        staged = keep.tile([4, PASSES, 4, N // 4], I32, align_bytes=256, name="staged")
         nc.scalar.dma_start(
             staged[:].rearrange("r a q n -> r (a q) n"),
             w_scales.bitcast(I32).rearrange("a (q r) n -> r (a q) n", r=4),
@@ -52,7 +52,7 @@ def tile_picked_pool_lin_relu_sub_e_kernel(tc, xT, w_words, w_scales, b, offs, o
                 packed[32 * q : 32 * q + 4, :].bitcast(word).rearrange("r (a n) -> r a n", a=PASSES),
                 staged[:].bitcast(word)[:, :, q, :],
             )
-        words = keep.tile([P, PASSES, N * 4], U8, align_bytes=64, name="words")
+        words = keep.tile([P, PASSES, N * 4], U8, align_bytes=256, name="words")
         lying = keep.tile([P, 64], F32, align_bytes=64, name="lying")
         standing = keep.tile([P, 64], F32, align_bytes=64, name="standing")
         nc.gpsimd.memset(lying[:], 0.0)
@@ -175,11 +175,11 @@ def tile_picked_pool_lin_relu_sub_e_kernel(tc, xT, w_words, w_scales, b, offs, o
                 op=mybir.AluOpType.max,
             )
             if i == 3:
-                early = keep.tile([P, 2, V // 2], F32, name="early")
+                early = keep.tile([P, 2, V // 2], F32, align_bytes=256, name="early")
                 for m in range(2):
                     nc.scalar.activation(early[:, m, :], best[:, m, 0 : V // 2], RELU, bias=bias[m])
                 nc.sync.dma_start(out.rearrange("(m p) v -> p m v", m=2)[:, :, 0 : V // 2], early[:])
-        late = [keep.tile([P, V // 2], F32, name="late%d" % m) for m in range(2)]
+        late = [keep.tile([P, V // 2], F32, align_bytes=256, name="late%d" % m) for m in range(2)]
         nc.scalar.activation(late[0][:], best[:, 0, V // 2 : V], RELU, bias=bias[0])
         nc.vector.tensor_scalar(
             late[1][:],

from contextlib import ExitStack

import concourse.mybir as mybir

K, T, S, V, D, N = 1024, 1024, 512, 128, 4, 256
P = 128
PACK = 4
PASSES = K // (P * PACK)
PIECE = 128
HALF = S // 2
PIECES = S // PIECE
LAST = PIECES - 1
FLOPS = 2 * K * S * N

F32 = mybir.dt.float32
BF16 = mybir.dt.bfloat16
U32 = mybir.dt.uint32
I32 = mybir.dt.int32
U16 = mybir.dt.uint16
U8 = mybir.dt.uint8
FP8X4 = mybir.dt.float8_e4m3fn_x4
COPY = mybir.ActivationFunctionType.Copy
RELU = mybir.ActivationFunctionType.Relu


def tile_picked_pool_lin_relu_sub_e_kernel(tc, xT, w_words, w_scales, b, offs, out):
    nc = tc.nc
    with ExitStack() as ctx:
        keep = ctx.enter_context(tc.tile_pool(name="keep", bufs=1))
        psum = ctx.enter_context(tc.psum_pool(name="psum", bufs=1))

        lists = keep.tile([P, S // 16], U16, name="lists")

        planes = xT.rearrange("(a p t) w -> a t p w", a=PASSES, t=PACK)
        plane = {}
        for a in range(PASSES):
            for t in range(PACK):
                x = keep.tile([P, T], F32, align_bytes=256, name="x%d%d" % (a, t))
                nc.sync.dma_start(x[:], planes[a, t])
                plane[a, t] = x[:]
                if (a, t) == (0, 0):
                    nc.sync.dma_start(lists[:], offs)
        staged = keep.tile([4, PASSES, 4, N // 4], I32, align_bytes=256, name="staged")
        nc.scalar.dma_start(
            staged[:].rearrange("r a q n -> r (a q) n"),
            w_scales.bitcast(I32).rearrange("a (q r) n -> r (a q) n", r=4),
        )
        packed = keep.tile([P, S], U8, align_bytes=64, name="packed")
        for q in range(4):
            copy, word = (nc.scalar.copy, U32) if q == 0 else (nc.vector.tensor_copy, I32)
            copy(
                packed[32 * q : 32 * q + 4, :].bitcast(word).rearrange("r (a n) -> r a n", a=PASSES),
                staged[:].bitcast(word)[:, :, q, :],
            )
        words = keep.tile([P, PASSES, N * 4], U8, align_bytes=256, name="words")
        lying = keep.tile([P, 64], F32, align_bytes=64, name="lying")
        standing = keep.tile([P, 64], F32, align_bytes=64, name="standing")
        nc.gpsimd.memset(lying[:], 0.0)
        nc.scalar.dma_start(
            lying[0:P:32, :].rearrange("q (m i) -> q m i", m=2),
            b.rearrange("(m q i) o -> q m (i o)", m=2, q=4),
        )
        for m in range(2):
            nc.vector.transpose(standing[:, 32 * m : 32 * m + 32], lying[:, 32 * m : 32 * m + 32])
        bias = [standing[:, 32 * m : 32 * m + 1] for m in range(2)]
        for a in range(PASSES):
            nc.sync.dma_start(words[:, a, :], w_words[a].rearrange("p n r -> p (n r)"))

        width = {0: HALF, 1: PIECE}
        grouped, codes, scales = {}, {}, {}
        for a in range(PASSES):
            for lo in range(0, S, width[a]):
                name = "grouped%d_%d" % (a, lo)
                grouped[a, lo] = keep.tile([P, width[a], PACK], BF16, align_bytes=64, name=name, tag=name)
                codes[a, lo] = keep.tile([P, width[a]], U32, align_bytes=64, name="codes%d_%d" % (a, lo))
                if a == 0:
                    scales[a, lo] = packed[4:, lo : lo + HALF]
                else:
                    scales[a, lo] = keep.tile([P, width[a]], U8, align_bytes=64, name="scales%d_%d" % (a, lo))[:]
        paired = [keep.tile([P, HALF // width[a], 2, width[a], 2], BF16, align_bytes=64, name="paired%d" % a) for a in range(PASSES)]
        rows0 = keep.tile([P, PACK, HALF], BF16, align_bytes=64, name="rows0")
        rows = [
            keep.tile([P, 1, 2, HALF], BF16, align_bytes=64, name="rows10"),
            keep.tile([P, HALF // PIECE, 2, PIECE], BF16, align_bytes=64, name="rows11"),
        ]
        banks = [((0, 0),), ((0, 1),), ((1, 0),), ((1, 1),), ((2, 0),), ((3, 0),), ((2, 1),), ((3, 1),)]
        bank = []
        for j, sums in enumerate(banks):
            bank.append(psum.tile([P, len(sums), PIECE], F32, name="bank%d" % j))

        def offsets(lo, hi):
            return lists[:, lo // 16 : hi // 16]

        def gather_pairs(a, t, lo=0, hi=HALF):
            w = width[a]
            nc.vector.tensor_copy(paired[a][:, lo // w : hi // w, t // 2, :, t % 2], plane[a, t].indirect(offsets(lo, hi)))

        def gather_rows(a, t):
            if a == 0:
                nc.scalar.activation(rows0[:, t, :], plane[a, t].indirect(offsets(HALF, S)), COPY)
                return
            tile = rows[t // 2]
            w = tile.shape[3]
            for j in range(HALF // w):
                lo = HALF + j * w
                nc.scalar.activation(tile[:, j, t % 2, :], plane[a, t].indirect(offsets(lo, lo + w)), COPY)

        def merge(a, lo):
            dst = grouped[a, lo][:].rearrange("p n t -> p (n t)").bitcast(U32).rearrange("p (n u) -> p n u", u=2)
            src = paired[a][:, lo // width[a]].rearrange("p u n e -> p (u n e)").bitcast(U32).rearrange("p (u n) -> p n u", u=2)
            nc.vector.tensor_copy(dst, src)

        def weave(u, lo, copy):
            tile = rows[u]
            j, c = divmod(lo - HALF, tile.shape[3])
            copy(grouped[1, lo][:, :, 2 * u : 2 * u + 2], tile[:, j, :, c : c + PIECE].rearrange("p e n -> p n e"))

        def quantize(a, lo):
            nc.vector.quantize_mx(
                out=codes[a, lo][:].bitcast(FP8X4),
                scales=scales[a, lo],
                in_=grouped[a, lo][:].rearrange("p n t -> p (n t)"),
            )

        def product(a, m, i, target, count, start, stop):
            base = i * PIECE // width[a] * width[a]
            cols = slice(i * PIECE - base, (i + count) * PIECE - base)
            nc.tensor.matmul_mx(
                out=target,
                lhsT=words[:, a, m * P * 4 : (m + 1) * P * 4].bitcast(FP8X4),
                lhsT_scale=packed[:, a * N + m * P : a * N + (m + 1) * P],
                rhs=codes[a, base][:, cols].bitcast(FP8X4),
                rhs_scale=scales[a, base][:, cols],
                start=start,
                stop=stop,
            )

        for a in range(PASSES):
            for t in range(PACK):
                if a == 1 and t == PACK - 1:
                    for lo in range(0, HALF, PIECE):
                        gather_pairs(a, t, lo, lo + PIECE)
                else:
                    gather_pairs(a, t)
                gather_rows(a, t)
                if a == 1 and t % 2 == 1:
                    for lo in range(HALF, S, PIECE):
                        weave(t // 2, lo, nc.vector.tensor_copy if (t, lo) == (1, S - PIECE) else nc.scalar.copy)
            for lo in range(0, HALF, width[a]):
                merge(a, lo)
            if a == 0:
                for lo, copy in ((0, nc.scalar.copy), (PIECE, nc.vector.tensor_copy)):
                    copy(
                        grouped[0, HALF][:, lo : lo + PIECE, :].rearrange("p (c i) t -> p c t i", i=4),
                        rows0[:, :, lo : lo + PIECE].rearrange("p t (c i) -> p c t i", i=4),
                    )
            for lo in range(0, S, width[a]):
                quantize(a, lo)
            for j, sums in enumerate(banks):
                if a == 0:
                    i, m = sums[0]
                    product(a, m, i, bank[j][:].rearrange("p c n -> p (c n)"), len(sums), True, False)
                else:
                    for c, (i, m) in enumerate(sums):
                        product(a, m, i, bank[j][:, c, :], 1, False, c == len(sums) - 1)

        best = keep.tile([P, 2, V], F32, align_bytes=64, name="best", tag="grouped1_%d" % ((LAST - 1) * PIECE))
        w = PIECE // D
        for i, sums in enumerate(banks):
            first, m = sums[0]
            nc.vector.tensor_reduce(
                best[:, m, first * w : (first + len(sums)) * w].rearrange("p (c v) -> p c v", c=len(sums)),
                bank[i][:].rearrange("p c (v d) -> p c v d", d=D),
                axis=mybir.AxisListType.X,
                op=mybir.AluOpType.max,
            )
            if i == 3:
                early = keep.tile([P, 2, V // 2], F32, align_bytes=256, name="early")
                for m in range(2):
                    nc.scalar.activation(early[:, m, :], best[:, m, 0 : V // 2], RELU, bias=bias[m])
                nc.sync.dma_start(out.rearrange("(m p) v -> p m v", m=2)[:, :, 0 : V // 2], early[:])
        late = [keep.tile([P, V // 2], F32, align_bytes=256, name="late%d" % m) for m in range(2)]
        nc.scalar.activation(late[0][:], best[:, 0, V // 2 : V], RELU, bias=bias[0])
        nc.vector.tensor_scalar(
            late[1][:],
            best[:, 1, V // 2 : V],
            scalar1=bias[1],
            scalar2=0.0,
            op0=mybir.AluOpType.add,
            op1=mybir.AluOpType.max,
        )
        for m in range(2):
            nc.sync.dma_start(out[m * P : (m + 1) * P, V // 2 : V], late[m][:])
